import numpy as np
import ml_dtypes


def mxq(x, axis, fmt="e4m3"):
    dtype, down = {"e4m3": (ml_dtypes.float8_e4m3fn, 7), "e5m2": (ml_dtypes.float8_e5m2, 14)}[fmt]
    v = np.moveaxis(np.asarray(x, np.float32).astype(ml_dtypes.bfloat16).astype(np.float64), axis, -1)
    blocks = v.reshape(v.shape[:-1] + (-1, 32))
    amax = np.abs(blocks).max(-1, keepdims=True)
    byte = np.maximum(np.where(amax > 0, np.frexp(amax)[1] - 1 + 127, 0) - down, 1)
    scale = np.exp2(byte - 127.0)
    codes = (blocks / scale).astype(np.float32).astype(dtype).astype(np.float64)
    return np.moveaxis((codes * scale).reshape(v.shape), -1, axis)


WIDE = False


def mx_kscale(k):
    if not WIDE:
        return np.ones(k)
    levels = np.array([10, -10, 5, -5, 0])
    if k % 512:
        return np.exp2(np.random.permutation(np.resize(levels, k // 32))).repeat(32)
    a = np.empty((k // 512, 16))
    for p in range(k // 512):
        a[p, :8] = np.random.permutation(np.resize(levels, 8))
        for g in range(8):
            far = levels[np.abs(levels - a[p, g]) >= 10]
            a[p, g + 8] = far[np.random.randint(len(far))]
    return np.exp2(a.ravel()).repeat(32)


BF16 = ml_dtypes.bfloat16


def bf(x):
    return np.asarray(x, np.float32).astype(BF16)


def f64(x):
    return np.asarray(x).astype(np.float64)


E2M1 = np.array([0.0, 0.5, 1.0, 1.5, 2.0, 3.0, 4.0, 6.0, -0.0, -0.5, -1.0, -1.5, -2.0, -3.0, -4.0, -6.0])


def pack_weight(w, fmt):
    k, n = w.shape
    w = f64(bf(w)).reshape(k // 32, 32, n)
    amax = np.abs(w).max(1)
    if fmt == "e4m3":
        byte = np.frexp(amax)[1] - 1 + 127 - 7
    else:
        mant, ex = np.frexp(amax / 6.0)
        byte = np.where(mant > 0.5, ex, ex - 1) + 127
    byte = np.clip(np.where(amax > 0, byte, 1), 1, 254)
    scaled = (w * np.exp2(127.0 - byte)[:, None, :]).reshape(k, n).astype(np.float32)
    by_word = np.ascontiguousarray(scaled.reshape(k // 512, 128, 4, n).transpose(0, 1, 3, 2))
    if fmt == "e4m3":
        words = by_word.astype(ml_dtypes.float8_e4m3fn).view(np.uint8)
    else:
        c = by_word.astype(ml_dtypes.float4_e2m1fn).view(np.uint8) & 0xF
        words = c[..., 0::2] | (c[..., 1::2] << 4)
    return np.ascontiguousarray(words), np.ascontiguousarray(byte.astype(np.uint8).reshape(k // 512, 16, n))


def unpack_weight(words, scales, fmt):
    g, p, n, _ = words.shape
    if fmt == "e4m3":
        vals = np.ascontiguousarray(words).view(ml_dtypes.float8_e4m3fn).astype(np.float64)
    else:
        nib = np.empty((g, p, n, 4), np.uint8)
        nib[..., 0::2] = words & 0xF
        nib[..., 1::2] = words >> 4
        vals = E2M1[nib]
    vals = vals * np.repeat(np.exp2(scales.astype(np.float64) - 127.0), 8, axis=1)[..., None]
    return vals.transpose(0, 1, 3, 2).reshape(g * 512, n)
def pack4(w):
    words, scales = pack_weight(w, "e2m1")
    return words.reshape(words.shape[0], 128, -1), scales


def unpack4(words, scales):
    return unpack_weight(words.reshape(words.shape[0], 128, -1, 2), scales, "e2m1")


B, O, T, C, E, N, D = 128, 2, 2, 512, 4, 512, 1024


def sigmoid(a):
    return 1.0 / (1.0 + np.exp(-a))


def setup_inputs():
    s, t = mx_kscale(C), mx_kscale(N)
    x = 0.7 * (np.random.standard_normal((B, 1, 1, C)) + np.random.standard_normal((B, O * T, O * T, C))) * s
    wr = 2.0 * np.random.standard_normal((C, E * N)) / np.sqrt(C) / s[:, None]
    we = np.random.standard_normal((T * T * C, E * N)) / np.sqrt(T * T * C) / np.tile(s, T * T)[:, None]
    wp = np.random.standard_normal((N, D)) / np.sqrt(N) / t[:, None]
    wr_words, wr_scales = pack4(wr)
    we_words, we_scales = pack4(we)
    wp_words, wp_scales = pack4(wp)
    return {"x": bf(x),
            "wr_words": wr_words, "wr_scales": wr_scales,
            "br": bf(0.5 * np.random.standard_normal(E * N)),
            "we_words": we_words, "we_scales": we_scales,
            "gain": bf((1.0 + 0.1 * np.random.standard_normal(N)) * t),
            "beta": bf(0.3 * np.random.standard_normal(N) * t),
            "wp_words": wp_words, "wp_scales": wp_scales,
            "bp": bf(0.3 * np.random.standard_normal(D))}


def reference(x, wr_words, wr_scales, br, we_words, we_scales, gain, beta, wp_words, wp_scales, bp):
    x = f64(x)
    pooled = x.mean(axis=(1, 2))
    logits = (mxq(pooled, 1, "e4m3") @ unpack4(wr_words, wr_scales)) + f64(br)
    r = sigmoid(logits).reshape(B, 1, E, N)
    patches = x.reshape(B, O, T, O, T, C).transpose(0, 1, 3, 2, 4, 5).reshape(B * O * O, T * T * C)
    y = (mxq(patches, 1, "e4m3") @ unpack4(we_words, we_scales)).reshape(B, O * O, E, N)
    m = (r * y).sum(axis=2).reshape(B * O * O, N)
    rms = np.sqrt((m * m).mean(axis=1, keepdims=True))
    h = np.maximum(m / rms * f64(gain) + f64(beta), 0.0)
    out = (mxq(h, 1, "e4m3") @ unpack4(wp_words, wp_scales)) + f64(bp)
    return out.reshape(B, O, O, D)

from contextlib import ExitStack

import concourse.mybir as mybir
from concourse.masks import make_identity

F32 = mybir.dt.float32
BF16 = mybir.dt.bfloat16
I32 = mybir.dt.int32
U32 = mybir.dt.uint32
U8 = mybir.dt.uint8
FP8X4 = mybir.dt.float8_e4m3fn_x4
FP4X4 = mybir.dt.float4_e2m1fn_x4
ACT = mybir.ActivationFunctionType
ALU = mybir.AluOpType

P = 128
B, C, E, N, D = 128, 512, 4, 512, 1024
EN = E * N
FLOPS = 2 * (B * C * EN + 4 * B * 4 * C * EN + 4 * B * N * D)


def tile_condconv_filter_routing_f1_kernel(
    tc, x, wr_words, wr_scales, br, we_words, we_scales, gain, beta, wp_words, wp_scales, bp, out
):
    nc = tc.nc
    with ExitStack() as ctx:
        keep = ctx.enter_context(tc.tile_pool(name="keep", bufs=1))
        work = ctx.enter_context(tc.tile_pool(name="work", bufs=3))
        psum = ctx.enter_context(tc.psum_pool(name="psum", bufs=4))
        ctx.enter_context(tc.manual_schedule())

        def kt(name, shape, dt):
            return keep.tile(shape, dt, name=name, align_bytes=64)

        def wt(name, shape, dt, bufs=3):
            return work.tile(shape, dt, name=name, tag=name, bufs=bufs, align_bytes=64)

        bank_counts = {"y": 4, "w": 2, "h": 2}

        def bank(tag, name):
            return psum.tile([P, 512], F32, name=name, tag=tag, bufs=bank_counts[tag])

        rows = kt("rows", [P, 512], BF16)
        one_col = kt("one_col", [P, 1], F32)
        dummy = kt("dummy", [P, 1], F32)
        neghalf = kt("neghalf", [P, 1], F32)
        id32 = kt("id32", [P, P], F32)
        id16 = kt("id16", [P, P], BF16)
        xs = [kt("xs%d" % q, [P, 2, 2 * C], BF16) for q in range(4)]
        xq = [kt("xq%d" % q, [P, 4, P], U32) for q in range(4)]
        xsc = [kt("xsc%d" % q, [P, 4, P], U8) for q in range(4)]
        wew = kt("wew", [P, 4, 2 * EN], U8)
        wesc = kt("wesc", [P, 4 * EN], U8)
        wrw = kt("wrw", [P, 2 * EN], U8)
        wrsc = kt("wrsc", [P, EN], U8)
        wpw = kt("wpw", [P, 2 * D], U8)
        wpsc = kt("wpsc", [P, D], U8)
        g16 = kt("g16", [P, 4], BF16)
        b16 = kt("b16", [P, 4], BF16)
        gcol = kt("gcol", [P, 4], F32)
        bcol = kt("bcol", [P, 4], F32)
        brb = kt("brb", [P, E, 4, P], BF16)
        bpb = kt("bpb", [P, D], BF16)
        pooled = kt("pooled", [P, C], BF16)
        pooledt = kt("pooledt", [P, C], BF16)
        pq = kt("pq", [P, P], U32)
        psc = kt("psc", [P, P], U8)
        rlin = kt("rlin", [P, E, 4, P], F32)
        r = kt("r", [P, E, 4, P], F32)

        nc.vector.memset(rows[:].bitcast(I32), 0)
        make_identity(nc, id32[:])
        nc.gpsimd.memset(one_col[:], 1.0)
        nc.gpsimd.memset(neghalf[:], -0.5)
        nc.vector.memset(wrsc[:].bitcast(I32), 0)
        nc.vector.memset(wesc[:].bitcast(I32), 0)
        nc.vector.tensor_copy(out=id16[:], in_=id32[:])
        nc.vector.memset(wpsc[:].bitcast(I32), 0)

        nc.scalar.dma_start(out=rows[0:E, :], in_=br.rearrange("(e n) -> e n", e=E))
        nc.scalar.dma_start(out=g16[:], in_=gain.rearrange("(p t) -> p t", t=4))
        nc.scalar.dma_start(out=b16[:], in_=beta.rearrange("(p t) -> p t", t=4))
        nc.scalar.activation(out=dummy[:], in_=one_col[:], func=ACT.Sigmoid)

        def load_x(q, i0, i1):
            u, v = divmod(q, 2)
            nc.sync.dma_start(
                out=xs[q][:, i0:i1, :].rearrange("p i (j c) -> p i j c", j=2),
                in_=x[:, 2 * u + i0 : 2 * u + i1, 2 * v : 2 * v + 2, :],
            )

        load_x(0, 0, 1)
        load_x(0, 1, 2)
        for q in range(1, 4):
            load_x(q, 0, 2)

        def load_scales(queue, plane, dram, n, passes):
            src = dram.bitcast(I32).rearrange("g (Q r) n -> r Q g n", r=4)
            for k in range(4):
                queue.dma_start(
                    out=plane[k:P:32, :].bitcast(I32).rearrange("p (g n) -> p g n", g=passes), in_=src[k]
                )

        def load_words(tile_ap, dram_ap):
            nc.sync.dma_start(out=tile_ap.bitcast(I32), in_=dram_ap.bitcast(I32))

        load_scales(nc.sync, wesc, we_scales, EN, 4)
        load_words(wew[:, 0, :], we_words[0])
        load_scales(nc.gpsimd, wrsc, wr_scales, EN, 1)
        load_words(wrw[:], wr_words[0])
        for g in range(1, 4):
            load_words(wew[:, g, :], we_words[g])
        load_words(wpw[:], wp_words[0])
        load_scales(nc.sync, wpsc, wp_scales, D, 1)
        nc.sync.dma_start(out=bpb[:], in_=bp.partition_broadcast(P))

        def spread_row(k, name):
            t = bank("w", name)
            nc.tensor.matmul(t[:], lhsT=id16[:, k : k + 1].to_broadcast([P, P]), rhs=rows[:], start=True, stop=True)
            return t

        def transpose_pair(q, i):
            t = bank("y", "xt%d%d" % (q, i))
            words = xs[q][:, i, :].bitcast(F32)
            for j in range(2):
                for s in range(2):
                    k = 2 * j + s
                    nc.tensor.transpose(
                        t[:, 128 * k : 128 * k + 128], words[:, 256 * j + s : 256 * (j + 1) : 2], id32[:]
                    )
            return t

        def copy_words(eng_copy, t, name, nj):
            g = wt(name, [P, 512 * nj], BF16)
            eng_copy(
                out=g[:].bitcast(F32).rearrange("p (j r s) -> p j r s", j=nj, s=2),
                in_=t[:, 0 : 256 * nj].rearrange("p (j s r) -> p j r s", j=nj, s=2),
            )
            return g

        def pool_pixel(acc, q, i, j, start, stop):
            nc.tensor.matmul(
                acc[:], lhsT=id16[:], rhs=xs[q][:, i, 512 * j : 512 * (j + 1)], start=start, stop=stop
            )

        def quant_pair(g, q, i):
            nc.vector.quantize_mx(
                out=xq[q][:, 2 * i : 2 * i + 2, :].rearrange("p g r -> p (g r)").bitcast(FP8X4),
                scales=xsc[q][:, 2 * i : 2 * i + 2, :].rearrange("p g r -> p (g r)"),
                in_=g[:],
            )

        def y_pass(acc, q, e, g):
            nc.tensor.matmul_mx(
                out=acc[:],
                lhsT=xq[q][:, g, :].bitcast(FP8X4),
                lhsT_scale=xsc[q][:, g, :],
                rhs=wew[:, g, 1024 * e : 1024 * (e + 1)].bitcast(FP4X4),
                rhs_scale=wesc[:, EN * g + 512 * e : EN * g + 512 * (e + 1)],
                start=(g == 0),
                stop=(g == 3),
            )

        def y_group(q, e):
            acc = bank("y", "y%d%d" % (q, e))
            for g in range(4):
                y_pass(acc, q, e, g)
            return acc

        def weigh(acc, q, e):
            p = wt("p", [P, 4, P], F32, bufs=8)
            nc.vector.tensor_tensor(
                out=p[:], in0=acc[:].rearrange("b (p t) -> b t p", t=4), in1=r[:, e], op=ALU.mult
            )
            return p

        def add(eng, a, b):
            s = wt("s", [P, 4, P], F32, bufs=4)
            eng.tensor_tensor(out=s[:], in0=a[:], in1=b[:], op=ALU.add)
            return s

        def square(m, cols=slice(0, P)):
            junk = wt("junk", [P, 4, P], BF16, bufs=2)
            ssq = wt("ssq", [P, 1], F32, bufs=4)
            nc.scalar.activation(
                out=junk[:, :, cols],
                in_=m[:, :, cols],
                func=ACT.Square,
                scale=N**-0.5,
                accum_out=ssq[:],
            )
            return ssq

        def rsqrt(ssq, bias=0.0):
            rinv = wt("rinv", [P, 1], F32, bufs=2)
            nc.scalar.activation(out=rinv[:], in_=ssq[:], func=ACT.Abs_reciprocal_sqrt, bias=bias)
            return rinv

        def norm(m):
            rinv = rsqrt(square(m))
            mn = wt("mn", [P, 4, P], F32, bufs=2)
            nc.scalar.activation(out=mn[:], in_=m[:], func=ACT.Copy, scale=rinv[:])
            return mn

        def transpose_h(mn, q):
            t = bank("h", "ht%d" % q)
            for k in range(4):
                nc.tensor.transpose(t[:, 128 * k : 128 * (k + 1)], mn[:, k, :], id32[:])
            return t

        def act_h(t):
            h = wt("h", [P, 4, P], BF16, bufs=2)
            for k in range(4):
                nc.scalar.activation(
                    out=h[:, k, :],
                    in_=t[:, 128 * k : 128 * (k + 1)],
                    func=ACT.Relu,
                    scale=gcol[:, k : k + 1],
                    bias=bcol[:, k : k + 1],
                )
            return h

        def interleave_h(h):
            hg = wt("hg", [P, 512], BF16, bufs=2)
            nc.vector.tensor_copy(
                out=hg[:].rearrange("p (b t) -> p b t", t=4), in_=h[:].rearrange("p t b -> p b t")
            )
            return hg

        def quant_h(hg):
            hq = wt("hq", [P, P], U32, bufs=2)
            hsc = wt("hsc", [P, P], U8, bufs=2)
            nc.vector.quantize_mx(out=hq[:].bitcast(FP8X4), scales=hsc[:], in_=hg[:])
            return hq, hsc

        def project(hq, hsc, q):
            banks = []
            for d in range(2):
                t = bank("w", "o%d%d" % (q, d))
                nc.tensor.matmul_mx(
                    out=t[:],
                    lhsT=hq[:].bitcast(FP8X4),
                    lhsT_scale=hsc[:],
                    rhs=wpw[:, 1024 * d : 1024 * (d + 1)].bitcast(FP4X4),
                    rhs_scale=wpsc[:, 512 * d : 512 * (d + 1)],
                    start=True,
                    stop=True,
                )
                banks.append(t)
            return banks

        def finish(banks, q, d):
            u, v = divmod(q, 2)
            o = wt("o", [P, 512], F32, bufs=8)
            nc.vector.tensor_tensor(
                out=o[:], in0=banks[d][:], in1=bpb[:, 512 * d : 512 * (d + 1)], op=ALU.add
            )
            nc.sync.dma_start(out=out[:, u, v, 512 * d : 512 * (d + 1)], in_=o[:])

        def br_copy(t, e):
            nc.scalar.copy(out=brb[:, e], in_=t[:].rearrange("b (p t) -> b t p", t=4))

        vsum = kt("vsum", [P, C], F32)

        def px(q, i, j):
            return xs[q][:, i, 512 * j : 512 * (j + 1)]

        def vadd(a, b):
            nc.vector.tensor_tensor(out=vsum[:], in0=a, in1=b, op=ALU.add)

        vcopy, scopy = nc.vector.tensor_copy, nc.scalar.copy

        tb = [spread_row(e, "br%d" % e) for e in range(2)]
        xt00 = transpose_pair(0, 0)
        xt01 = transpose_pair(0, 1)
        vadd(px(0, 0, 0), px(0, 0, 1))
        g00 = copy_words(vcopy, xt00, "xg", 2)
        br_copy(tb[0], 0)
        g01 = copy_words(scopy, xt01, "xg", 2)
        br_copy(tb[1], 1)
        vadd(vsum[:], px(0, 1, 0))
        quant_pair(g00, 0, 0)
        vcopy(out=gcol[:], in_=g16[:])
        vcopy(out=bcol[:], in_=b16[:])
        vadd(vsum[:], px(0, 1, 1))
        quant_pair(g01, 0, 1)
        xt10 = transpose_pair(1, 0)
        xt11 = transpose_pair(1, 1)
        tb += [spread_row(e, "br%d" % e) for e in range(2, 4)]
        g10 = copy_words(scopy, xt10, "xg", 2)
        vadd(vsum[:], px(1, 0, 0))
        g11 = copy_words(scopy, xt11, "xg", 2)
        br_copy(tb[2], 2)
        br_copy(tb[3], 3)
        vadd(vsum[:], px(1, 0, 1))
        quant_pair(g10, 1, 0)
        vadd(vsum[:], px(1, 1, 0))
        quant_pair(g11, 1, 1)
        vadd(vsum[:], px(1, 1, 1))
        acc_pool = bank("h", "pool")
        for q in (2, 3):
            xta = transpose_pair(q, 0)
            xtb = transpose_pair(q, 1)
            for k in range(4):
                pool_pixel(acc_pool, q, k // 2, k % 2, q == 2 and k == 0, q == 3 and k == 3)
            ga = copy_words(vcopy, xta, "xg", 2)
            gb = copy_words(scopy, xtb, "xg", 2)
            quant_pair(ga, q, 0)
            quant_pair(gb, q, 1)
        nc.vector.tensor_tensor(out=pooled[:], in0=acc_pool[:], in1=vsum[:], op=ALU.add)

        y0 = [bank("y", "y0%d" % e) for e in range(E)]
        for e in range(E):
            y_pass(y0[e], 0, e, 0)
        t = bank("h", "pt")
        pw = pooled[:].bitcast(F32)
        for s in range(2):
            nc.tensor.transpose(t[:, 128 * s : 128 * (s + 1)], pw[:, s:256:2], id32[:])
        nc.vector.tensor_copy(
            out=pooledt[:].bitcast(F32).rearrange("p (r s) -> p r s", s=2),
            in_=t[:, 0:256].rearrange("p (s r) -> p r s", s=2),
        )
        nc.vector.quantize_mx(out=pq[:].bitcast(FP8X4), scales=psc[:], in_=pooledt[:])
        for e in range(E):
            y_pass(y0[e], 0, e, 1)

        def route(e):
            t = bank("w", "lg%d" % e)
            nc.tensor.matmul_mx(
                out=t[:],
                lhsT=pq[:].bitcast(FP8X4),
                lhsT_scale=psc[:],
                rhs=wrw[:, 1024 * e : 1024 * (e + 1)].bitcast(FP4X4),
                rhs_scale=wrsc[:, 512 * e : 512 * (e + 1)],
                start=True,
                stop=True,
            )
            nc.vector.scalar_tensor_tensor(
                out=rlin[:, e],
                in0=t[:].rearrange("b (p t) -> b t p", t=4),
                scalar=1.0 / 16,
                in1=brb[:, e],
                op0=ALU.mult,
                op1=ALU.add,
            )
            nc.scalar.activation(out=r[:, e], in_=rlin[:, e], func=ACT.Sigmoid)

        route(0)
        route(1)
        for e in range(E):
            y_pass(y0[e], 0, e, 2)
        route(2)
        route(3)
        for e in range(E):
            y_pass(y0[e], 0, e, 3)

        def mix(accs, q, es, m, last=True):
            for e in es:
                p = weigh(accs[e], q, e)
                if m is None:
                    m = p
                elif e < 3:
                    m = add(nc.gpsimd, m, p)
                else:
                    m = (m, p)
            return m

        def total(m):
            return add(nc.vector, *m)

        def fill(h):
            return quant_h(interleave_h(h))

        m0 = total(mix(y0, 0, range(4), None))
        y1 = [y_group(1, e) for e in range(4)]
        mn0 = norm(m0)
        t0 = transpose_h(mn0, 0)
        m1 = total(mix(y1, 1, range(4), None))
        h0 = act_h(t0)
        hq0 = fill(h0)
        y2 = [y_group(2, e) for e in range(2)]
        o0 = project(*hq0, 0)
        y2 += [y_group(2, e) for e in range(2, 3)]
        mn1 = norm(m1)
        t1 = transpose_h(mn1, 1)
        y2.append(y_group(2, 3))
        m2 = mix(y2, 2, range(1), None)
        finish(o0, 0, 0)
        m2 = mix(y2, 2, range(1, 2), m2)
        finish(o0, 0, 1)
        m2 = mix(y2, 2, range(2, 3), m2)
        h1 = act_h(t1)
        hq1 = fill(h1)
        m2 = total(mix(y2, 2, range(3, 4), m2))
        y3 = [y_group(3, 0)]
        y3.append(y_group(3, 1))
        m3 = mix(y3, 3, range(2), None)
        o1 = project(*hq1, 1)
        y3.append(y_group(3, 2))
        finish(o1, 1, 0)
        finish(o1, 1, 1)
        p32 = weigh(y3[2], 3, 2)
        mn2 = norm(m2)
        y3h = []
        for half in range(2):
            acc = bank("y", "y33%d" % half)
            for c in range(2):
                f0 = 256 * half + 128 * c
                for g in range(4):
                    nc.tensor.matmul_mx(
                        out=acc[:, 128 * c : 128 * (c + 1)],
                        lhsT=xq[3][:, g, :].bitcast(FP8X4),
                        lhsT_scale=xsc[3][:, g, :],
                        rhs=wew[:, g, 1024 * 3 + 2 * f0 : 1024 * 3 + 2 * f0 + 256].bitcast(FP4X4),
                        rhs_scale=wesc[:, EN * g + 512 * 3 + f0 : EN * g + 512 * 3 + f0 + 128],
                        start=(g == 0),
                        stop=(g == 3),
                    )
            y3h.append(acc)
        t2 = transpose_h(mn2, 2)
        h2 = act_h(t2)
        p3 = wt("p", [P, 4, P], F32, bufs=8)
        s3 = wt("s", [P, 4, P], F32, bufs=4)
        halves = [slice(0, 64), slice(64, 128)]

        def weigh_half(k):
            nc.vector.tensor_tensor(
                out=p3[:, :, halves[k]],
                in0=y3h[k][:, 0:256].rearrange("b (p t) -> b t p", t=4),
                in1=r[:, 3, :, halves[k]],
                op=ALU.mult,
            )

        def add_half(k):
            nc.vector.tensor_tensor(
                out=s3[:, :, halves[k]], in0=m3[:, :, halves[k]], in1=p3[:, :, halves[k]], op=ALU.add
            )

        weigh_half(0)
        m3 = add(nc.vector, m3, p32)
        weigh_half(1)
        add_half(0)
        add_half(1)
        ssq = [square(s3, halves[k]) for k in range(2)]
        mn3 = wt("mn", [P, 4, P], F32, bufs=2)
        rinv = rsqrt(ssq[0], bias=ssq[1][:])
        nc.vector.tensor_scalar(out=mn3[:, 0:2], in0=s3[:, 0:2], scalar1=rinv[:], scalar2=None, op0=ALU.mult)
        nc.vector.tensor_scalar(out=mn3[:, 2:4], in0=s3[:, 2:4], scalar1=rinv[:], scalar2=None, op0=ALU.mult)
        hq2 = fill(h2)
        t3 = [bank("h", "ht3%d" % k) for k in range(2)]
        for k in range(4):
            nc.tensor.transpose(t3[k // 2][:, 128 * (k % 2) : 128 * (k % 2 + 1)], mn3[:, k, :], id32[:])
        h3 = wt("h", [P, 4, P], BF16, bufs=2)
        for k in range(4):
            src = t3[k // 2][:, 128 * (k % 2) : 128 * (k % 2 + 1)]
            if k < 2:
                nc.scalar.activation(
                    out=h3[:, k, :], in_=src, func=ACT.Identity, scale=gcol[:, k : k + 1], bias=bcol[:, k : k + 1]
                )
            else:
                nc.vector.tensor_scalar(
                    out=h3[:, k, :],
                    in0=src,
                    scalar1=gcol[:, k : k + 1],
                    scalar2=bcol[:, k : k + 1],
                    op0=ALU.mult,
                    op1=ALU.add,
                )
        hg3 = wt("hg", [P, 512], BF16, bufs=2)
        nc.vector.tensor_scalar(
            out=hg3[:].rearrange("p (b t) -> p b t", t=4),
            in0=h3[:].rearrange("p t b -> p b t"),
            scalar1=0.0,
            scalar2=None,
            op0=ALU.max,
        )
        o2 = project(*hq2, 2)
        hq3 = quant_h(hg3)
        o3 = project(*hq3, 3)
        finish(o2, 2, 0)
        finish(o2, 2, 1)
        finish(o3, 3, 0)
        finish(o3, 3, 1)
